import numpy as np
import ml_dtypes


def mxq(x, axis, fmt="e4m3"):
    dtype, down = {"e4m3": (ml_dtypes.float8_e4m3fn, 7), "e5m2": (ml_dtypes.float8_e5m2, 14)}[fmt]
    v = np.moveaxis(np.asarray(x, np.float32).astype(ml_dtypes.bfloat16).astype(np.float64), axis, -1)
    blocks = v.reshape(v.shape[:-1] + (-1, 32))
    amax = np.abs(blocks).max(-1, keepdims=True)
    byte = np.maximum(np.where(amax > 0, np.frexp(amax)[1] - 1 + 127, 0) - down, 1)
    scale = np.exp2(byte - 127.0)
    codes = (blocks / scale).astype(np.float32).astype(dtype).astype(np.float64)
    return np.moveaxis((codes * scale).reshape(v.shape), -1, axis)


WIDE = False


def mx_kscale(k):
    if not WIDE:
        return np.ones(k)
    levels = np.array([10, -10, 5, -5, 0])
    if k % 512:
        return np.exp2(np.random.permutation(np.resize(levels, k // 32))).repeat(32)
    a = np.empty((k // 512, 16))
    for p in range(k // 512):
        a[p, :8] = np.random.permutation(np.resize(levels, 8))
        for g in range(8):
            far = levels[np.abs(levels - a[p, g]) >= 10]
            a[p, g + 8] = far[np.random.randint(len(far))]
    return np.exp2(a.ravel()).repeat(32)


def f64(x):
    return np.asarray(x).astype(np.float64)


def striped(idx):
    return np.tile(idx.reshape(-1, 16).T, (8, 1)).astype(np.uint16)


def unstriped(offs):
    return offs[:16].T.reshape(-1).astype(np.int64)


def pack_weight(w):
    k, n = w.shape
    w = f64(np.asarray(w, np.float32).astype(ml_dtypes.bfloat16)).reshape(k // 32, 32, n)
    amax = np.abs(w).max(1)
    byte = np.clip(np.where(amax > 0, np.frexp(amax)[1] - 1 + 127 - 7, 1), 1, 254)
    scaled = (w * np.exp2(127.0 - byte)[:, None, :]).reshape(k, n).astype(np.float32)
    words = np.ascontiguousarray(scaled.reshape(k // 512, 128, 4, n).transpose(0, 1, 3, 2)).astype(ml_dtypes.float8_e4m3fn).view(np.uint8)
    return words, np.ascontiguousarray(byte.astype(np.uint8).reshape(k // 512, 16, n))


def unpack_weight(words, scales):
    g, p, n, _ = words.shape
    vals = np.ascontiguousarray(words).view(ml_dtypes.float8_e4m3fn).astype(np.float64) * np.repeat(np.exp2(scales.astype(np.float64) - 127.0), 8, axis=1)[..., None]
    return vals.transpose(0, 1, 3, 2).reshape(g * 512, n)


E2M1 = np.array([0.0, 0.5, 1.0, 1.5, 2.0, 3.0, 4.0, 6.0, -0.0, -0.5, -1.0, -1.5, -2.0, -3.0, -4.0, -6.0])


def pack_fp4(w):
    k, n = w.shape
    w = f64(np.asarray(w, np.float32).astype(ml_dtypes.bfloat16)).reshape(k // 32, 32, n)
    amax = np.abs(w).max(1)
    mant, ex = np.frexp(amax / 6.0)
    byte = np.clip(np.where(amax > 0, np.where(mant > 0.5, ex, ex - 1) + 127, 1), 1, 254)
    scaled = (w * np.exp2(127.0 - byte)[:, None, :]).reshape(k, n).astype(np.float32)
    c = np.ascontiguousarray(scaled.reshape(k // 512, 128, 4, n).transpose(0, 1, 3, 2)).astype(ml_dtypes.float4_e2m1fn).view(np.uint8) & 0xF
    words = (c[..., 0::2] | (c[..., 1::2] << 4)).reshape(k // 512, 128, 2 * n)
    return np.ascontiguousarray(words), np.ascontiguousarray(byte.astype(np.uint8).reshape(k // 512, 16, n))


def unpack_fp4(words, scales):
    g, _, n = scales.shape
    words = np.ascontiguousarray(words).reshape(g, 128, n, 2)
    nib = np.empty((g, 128, n, 4), np.uint8)
    nib[..., 0::2] = words & 0xF
    nib[..., 1::2] = words >> 4
    vals = E2M1[nib] * np.repeat(np.exp2(scales.astype(np.float64) - 127.0), 8, axis=1)[..., None]
    return vals.transpose(0, 1, 3, 2).reshape(g * 512, n)


K, T, S, D, N, H, V, U = 512, 2048, 512, 2, 128, 512, 256, 512


def setup_inputs():
    n = np.random.standard_normal
    s = mx_kscale(K)[:, None]
    u = mx_kscale(H)
    packed_xT = pack_weight(n((K, T)) * s)
    packed_w1 = pack_fp4(n((K, H)) / np.sqrt(K) / s)
    packed_w2 = pack_fp4(n((H, N)) / np.sqrt(H) / u[:, None])
    return {
        "x_words": packed_xT[0],
        "x_scales": packed_xT[1],
        "w1_words": packed_w1[0],
        "w1_scales": packed_w1[1],
        "sg": (np.where(np.random.uniform(size=(H, S)) < 0.5, -1.0, 1.0) * np.random.uniform(0.7, 1.3, (H, S))).astype(np.float32),
        "unit": (np.random.uniform(0.6, 1.4, (H, 1)) * u[:, None]).astype(np.float32),
        "w2_words": packed_w2[0],
        "w2_scales": packed_w2[1],
        "offs": striped(np.random.permutation(T)[:S]),
        "ra": striped(np.random.permutation(np.concatenate([np.arange(V), np.random.randint(0, V, U - V)]))),
        "rb": striped(np.random.permutation(np.concatenate([np.arange(V), np.random.randint(0, V, U - V)]))),
    }


def reference(x_words, x_scales, w1_words, w1_scales, sg, unit, w2_words, w2_scales, offs, ra, rb):
    xq = unpack_weight(x_words, x_scales)[:, unstriped(offs)]
    y = unpack_fp4(w1_words, w1_scales).T @ xq
    hsum = y.reshape(len(y), -1, D).sum(axis=2)
    ea = hsum[:, unstriped(ra)]
    ys_ = y * f64(sg)
    hdif = ys_.reshape(len(ys_), -1, D).sum(axis=2)
    eb = hdif[:, unstriped(rb)]
    rot1 = ea + eb
    rot2 = hsum[:, unstriped(rb)] - hdif[:, unstriped(ra)]
    absm = np.maximum(np.abs(rot1), np.abs(rot2))
    hid = f64(unit) * (rot1 * rot2 - absm)
    return unpack_fp4(w2_words, w2_scales).T @ mxq(hid, 0, "e4m3")

@@ -1,0 +1,169 @@
+from contextlib import ExitStack
+
+import concourse.mybir as mybir
+
+K, T, S, N, H, V = 512, 2048, 512, 128, 512, 256
+FLOPS = 2 * K * H * S + 2 * H * N * S
+
+F32 = mybir.dt.float32
+BF16 = mybir.dt.bfloat16
+I32 = mybir.dt.int32
+U32 = mybir.dt.uint32
+U16 = mybir.dt.uint16
+U8 = mybir.dt.uint8
+FP8X4 = mybir.dt.float8_e4m3fn_x4
+FP4X4 = mybir.dt.float4_e2m1fn_x4
+ALU = mybir.AluOpType
+ACT = mybir.ActivationFunctionType
+
+P = 128
+PACK = 4
+CHUNKS = [(0, 256), (256, 256)]
+
+
+def load_scale_rows(queue, plane, rows):
+    for q in range(4):
+        queue.dma_start(out=plane[32 * q : 32 * q + 4, :].bitcast(I32), in_=rows[4 * q : 4 * q + 4, :].bitcast(I32))
+
+
+def tile_picked_yrotqv_mul_p_kernel(
+    tc, x_words, x_scales, w1_words, w1_scales, sg, unit, w2_words, w2_scales, offs, ra, rb, out
+):
+    nc = tc.nc
+    with ExitStack() as ctx:
+        keep = ctx.enter_context(tc.tile_pool(name="keep", bufs=1))
+        psum = ctx.enter_context(tc.psum_pool(name="psum", bufs=1))
+
+        offs_t = keep.tile([P, S // 16], U16, name="offs_t")
+        ra_t = keep.tile([P, S // 16], U16, name="ra_t")
+        rb_t = keep.tile([P, S // 16], U16, name="rb_t")
+        xw = keep.tile([P, T], U32, name="xw", align_bytes=64)
+        xs = keep.tile([P, T], U8, name="xs", align_bytes=64)
+        w1w = keep.tile([P, 2 * H], U8, name="w1w", align_bytes=64)
+        w1s = keep.tile([P, H], U8, name="w1s", align_bytes=64)
+        w2w = keep.tile([P, 2 * N], U8, name="w2w", align_bytes=64)
+        w2s = keep.tile([P, N], U8, name="w2s", align_bytes=64)
+        gains = [keep.tile([P, S], F32, name="gain%d" % t) for t in range(PACK)]
+        u = keep.tile([P, PACK], F32, name="u")
+        neg_u = keep.tile([P, PACK], F32, name="neg_u")
+
+        nc.gpsimd.memset(xs[:].bitcast(I32), 0)
+        nc.vector.memset(w1s[:].bitcast(I32), 0)
+        nc.gpsimd.memset(w2s[:].bitcast(I32), 0)
+
+        nc.sync.dma_start(out=w1w[:].bitcast(I32), in_=w1_words[0].bitcast(I32))
+        nc.sync.dma_start(offs_t[:], offs)
+        load_scale_rows(nc.sync, xs, x_scales[0])
+        nc.sync.dma_start(out=xw[:].bitcast(I32), in_=x_words[0].rearrange("p n t -> p (n t)").bitcast(I32))
+        load_scale_rows(nc.sync, w1s, w1_scales[0])
+        sg_rows = sg.rearrange("(p t) j -> p t j", t=PACK)
+        for t in range(PACK):
+            nc.sync.dma_start(out=gains[t][:], in_=sg_rows[:, t, :])
+        nc.sync.dma_start(ra_t[:], ra)
+        nc.sync.dma_start(rb_t[:], rb)
+        nc.sync.dma_start(out=u[:], in_=unit.rearrange("(p t) o -> p (t o)", t=PACK))
+        nc.sync.dma_start(out=w2w[:].bitcast(I32), in_=w2_words[0].bitcast(I32))
+        load_scale_rows(nc.sync, w2s, w2_scales[0])
+
+        nc.scalar.activation(neg_u[:], u[:], ACT.Copy, scale=-1.0)
+
+        w1w_dealt = keep.tile([P, 2 * H], U8, name="w1w_dealt", align_bytes=64)
+        w1s_dealt = keep.tile([P, H], U8, name="w1s_dealt", align_bytes=64)
+        nc.vector.tensor_copy(
+            out=w1w_dealt[:].rearrange("p (t m b) -> p t m b", t=PACK, b=2),
+            in_=w1w[:].rearrange("p (m t b) -> p t m b", t=PACK, b=2),
+        )
+        picked_s = keep.tile([P, S], U8, name="picked_s", align_bytes=64)
+        picked_w = keep.tile([P, S], U32, name="picked_w", align_bytes=64)
+        nc.vector.tensor_copy(picked_s[:], xs[:].indirect(offs_t[:]))
+        nc.vector.tensor_copy(
+            out=w1s_dealt[:].rearrange("p (t m) -> p t m", t=PACK),
+            in_=w1s[:].rearrange("p (m t) -> p t m", t=PACK),
+        )
+        nc.vector.tensor_copy(picked_w[:], xw[:].indirect(offs_t[:]))
+
+        sum_tab, dif_tab = [], []
+        for t in range(PACK):
+            y = psum.tile([P, S], F32, name="y%d" % t)
+            nc.tensor.matmul_mx(
+                out=y[:],
+                lhsT=w1w_dealt[:, 2 * P * t : 2 * P * (t + 1)].bitcast(FP4X4),
+                lhsT_scale=w1s_dealt[:, P * t : P * (t + 1)],
+                rhs=picked_w[:].bitcast(FP8X4),
+                rhs_scale=picked_s[:],
+                start=True,
+                stop=True,
+            )
+            st = keep.tile([P, V + S], F32, name="sum_tab%d" % t)
+            dt_ = keep.tile([P, V + S], F32, name="dif_tab%d" % t)
+            nc.scalar.activation(st[:, V:], y[:], ACT.Copy)
+            nc.vector.tensor_tensor(dt_[:, V:], y[:], gains[t][:], ALU.mult)
+            nc.vector.tensor_tensor(st[:, :V], st[:, V :: 2], st[:, V + 1 :: 2], ALU.add)
+            nc.vector.tensor_tensor(dt_[:, :V], dt_[:, V :: 2], dt_[:, V + 1 :: 2], ALU.add)
+            sum_tab.append(st)
+            dif_tab.append(dt_)
+
+        steps = [(c, t) for c in range(len(CHUNKS)) for t in range(PACK)]
+        rot, mag, hid = {}, {}, {}
+
+        def lists(c):
+            j0, w = CHUNKS[c]
+            return ra_t[:, j0 // 16 : (j0 + w) // 16], rb_t[:, j0 // 16 : (j0 + w) // 16]
+
+        def fetch(c, t):
+            w = CHUNKS[c][1]
+            a, b = lists(c)
+            first = keep.tile([P, 2, w], F32, name="first%d_%d" % (c, t))
+            nc.scalar.activation(first[:, 0, :], sum_tab[t][:].indirect(a), ACT.Copy)
+            nc.scalar.activation(first[:, 1, :], dif_tab[t][:].indirect(a), ACT.Copy)
+            r = keep.tile([P, 2, w], F32, name="rot%d_%d" % (c, t))
+            nc.vector.tensor_tensor(r[:, 0, :], dif_tab[t][:].indirect(b), first[:, 0, :], ALU.add)
+            nc.vector.tensor_tensor(r[:, 1, :], sum_tab[t][:].indirect(b), first[:, 1, :], ALU.subtract)
+            rot[c, t] = r
+
+        def combine(c, t):
+            w = CHUNKS[c][1]
+            r = rot[c, t]
+            a = keep.tile([P, 2, w], F32, name="abs%d_%d" % (c, t))
+            nc.scalar.activation(a[:], r[:], ACT.Abs)
+            prod = keep.tile([P, w], F32, name="prod%d_%d" % (c, t))
+            nc.vector.scalar_tensor_tensor(prod[:], r[:, 0, :], u[:, t : t + 1], r[:, 1, :], ALU.mult, ALU.mult)
+            m = keep.tile([P, w], F32, name="max%d_%d" % (c, t))
+            nc.vector.tensor_tensor(m[:], a[:, 0, :], a[:, 1, :], ALU.max)
+            if t == 0:
+                hid[c] = keep.tile([P, PACK, w], BF16, name="hid%d" % c)
+            nc.vector.scalar_tensor_tensor(hid[c][:, t, :], m[:], neg_u[:, t : t + 1], prod[:], ALU.mult, ALU.add)
+
+        def finish(c):
+            j0, w = CHUNKS[c]
+            woven = keep.tile([P, w, PACK], BF16, name="woven%d" % c, align_bytes=64)
+            nc.scalar.copy(
+                out=woven[:].rearrange("p (c i) t -> p c t i", i=4),
+                in_=hid[c][:].rearrange("p t (c i) -> p c t i", i=4),
+            )
+            codes = keep.tile([P, w], U32, name="codes%d" % c, align_bytes=64)
+            scales = keep.tile([P, w], U8, name="scales%d" % c, align_bytes=64)
+            nc.vector.quantize_mx(
+                out=codes[:].bitcast(FP8X4), scales=scales[:], in_=woven[:].rearrange("p w t -> p (w t)")
+            )
+            acc = psum.tile([P, w], F32, name="acc%d" % c)
+            nc.tensor.matmul_mx(
+                out=acc[:],
+                lhsT=w2w[:].bitcast(FP4X4),
+                lhsT_scale=w2s[:],
+                rhs=codes[:].bitcast(FP8X4),
+                rhs_scale=scales[:],
+                start=True,
+                stop=True,
+            )
+            res = keep.tile([P, w], F32, name="res%d" % c)
+            nc.scalar.activation(res[:], acc[:], ACT.Copy)
+            nc.sync.dma_start(out=out[:, j0 : j0 + w], in_=res[:])
+
+        for i in range(len(steps) + 2):
+            if i < len(steps):
+                fetch(*steps[i])
+            if 1 <= i <= len(steps):
+                combine(*steps[i - 1])
+            if i >= 2 and steps[i - 2][1] == PACK - 1:
+                finish(steps[i - 2][0])

@@ -18,7 +18,9 @@ ACT = mybir.ActivationFunctionType
 
 P = 128
 PACK = 4
-CHUNKS = [(0, 256), (256, 256)]
+CHUNKS = [(0, 384), (384, 128)]
+TINY = 1e-30
+ON_VECTOR = [(0, 0)]
 
 
 def load_scale_rows(queue, plane, rows):
@@ -45,9 +47,9 @@ def tile_picked_yrotqv_mul_p_kernel(
         w2s = keep.tile([P, N], U8, name="w2s", align_bytes=64)
         gains = [keep.tile([P, S], F32, name="gain%d" % t) for t in range(PACK)]
         u = keep.tile([P, PACK], F32, name="u")
-        neg_u = keep.tile([P, PACK], F32, name="neg_u")
 
-        nc.gpsimd.memset(xs[:].bitcast(I32), 0)
+        nc.vector.memset(xs[:, : T // 2].bitcast(I32), 0)
+        nc.gpsimd.memset(xs[:, T // 2 :].bitcast(I32), 0)
         nc.vector.memset(w1s[:].bitcast(I32), 0)
         nc.gpsimd.memset(w2s[:].bitcast(I32), 0)
 
@@ -56,16 +58,34 @@ def tile_picked_yrotqv_mul_p_kernel(
         load_scale_rows(nc.sync, xs, x_scales[0])
         nc.sync.dma_start(out=xw[:].bitcast(I32), in_=x_words[0].rearrange("p n t -> p (n t)").bitcast(I32))
         load_scale_rows(nc.sync, w1s, w1_scales[0])
+        nc.sync.dma_start(out=u[:], in_=unit.rearrange("(p t) o -> p (t o)", t=PACK))
         sg_rows = sg.rearrange("(p t) j -> p t j", t=PACK)
         for t in range(PACK):
             nc.sync.dma_start(out=gains[t][:], in_=sg_rows[:, t, :])
         nc.sync.dma_start(ra_t[:], ra)
         nc.sync.dma_start(rb_t[:], rb)
-        nc.sync.dma_start(out=u[:], in_=unit.rearrange("(p t) o -> p (t o)", t=PACK))
         nc.sync.dma_start(out=w2w[:].bitcast(I32), in_=w2_words[0].bitcast(I32))
         load_scale_rows(nc.sync, w2s, w2_scales[0])
 
-        nc.scalar.activation(neg_u[:], u[:], ACT.Copy, scale=-1.0)
+        mag_u = keep.tile([P, PACK], F32, name="mag_u")
+        root0 = keep.tile([P, PACK], F32, name="root0")
+        sign_u = keep.tile([P, PACK], F32, name="sign_u")
+        inv = keep.tile([P, PACK], F32, name="inv")
+        quot = keep.tile([P, PACK], F32, name="quot")
+        half_root = keep.tile([P, PACK], F32, name="half_root")
+        bias_x = keep.tile([P, PACK], F32, name="bias_x")
+        bias_y = keep.tile([P, PACK], F32, name="bias_y")
+        nc.gpsimd.tensor_scalar(mag_u[:], u[:], 0.0, 2.0, ALU.is_ge, ALU.mult)
+        nc.gpsimd.tensor_scalar(sign_u[:], mag_u[:], 1.0, -1.0, ALU.mult, ALU.add)
+        nc.gpsimd.tensor_tensor(mag_u[:], u[:], sign_u[:], ALU.mult)
+        nc.scalar.activation(root0[:], mag_u[:], ACT.Sqrt)
+        nc.gpsimd.tensor_scalar(inv[:], root0[:], TINY, None, ALU.max)
+        nc.vector.reciprocal(inv[:], inv[:])
+        nc.gpsimd.tensor_tensor(quot[:], mag_u[:], inv[:], ALU.mult)
+        nc.gpsimd.tensor_tensor(quot[:], quot[:], root0[:], ALU.add)
+        nc.gpsimd.tensor_scalar(half_root[:], quot[:], 0.25, None, ALU.mult)
+        nc.gpsimd.tensor_tensor(bias_y[:], half_root[:], sign_u[:], ALU.mult)
+        nc.gpsimd.tensor_scalar(bias_x[:], bias_y[:], -1.0, None, ALU.mult)
 
         w1w_dealt = keep.tile([P, 2 * H], U8, name="w1w_dealt", align_bytes=64)
         w1s_dealt = keep.tile([P, H], U8, name="w1s_dealt", align_bytes=64)
@@ -76,70 +96,99 @@ def tile_picked_yrotqv_mul_p_kernel(
         picked_s = keep.tile([P, S], U8, name="picked_s", align_bytes=64)
         picked_w = keep.tile([P, S], U32, name="picked_w", align_bytes=64)
         nc.vector.tensor_copy(picked_s[:], xs[:].indirect(offs_t[:]))
-        nc.vector.tensor_copy(
-            out=w1s_dealt[:].rearrange("p (t m) -> p t m", t=PACK),
-            in_=w1s[:].rearrange("p (m t) -> p t m", t=PACK),
-        )
-        nc.vector.tensor_copy(picked_w[:], xw[:].indirect(offs_t[:]))
+        dealt_view = w1s_dealt[:].rearrange("p (t m) -> p t m", t=PACK)
+        raw_view = w1s[:].rearrange("p (m t) -> p t m", t=PACK)
+        HALF = S // 2
+        nc.vector.tensor_copy(picked_w[:, :HALF], xw[:].indirect(offs_t[:, : HALF // 16]))
+        nc.vector.tensor_copy(out=dealt_view[:, 0, :], in_=raw_view[:, 0, :])
+        nc.vector.tensor_copy(picked_w[:, HALF:], xw[:].indirect(offs_t[:, HALF // 16 :]))
+        nc.vector.tensor_copy(out=dealt_view[:, 1:, :], in_=raw_view[:, 1:, :])
 
-        sum_tab, dif_tab = [], []
+        shift_x = keep.tile([P, PACK], F32, name="shift_x")
+        shift_y = keep.tile([P, PACK], F32, name="shift_y")
+        nc.gpsimd.tensor_scalar(shift_y[:], bias_y[:], 2.0, None, ALU.mult)
+        nc.gpsimd.tensor_scalar(shift_x[:], bias_y[:], -2.0, None, ALU.mult)
+
+        w_tab, b_tab = [], []
         for t in range(PACK):
-            y = psum.tile([P, S], F32, name="y%d" % t)
-            nc.tensor.matmul_mx(
-                out=y[:],
-                lhsT=w1w_dealt[:, 2 * P * t : 2 * P * (t + 1)].bitcast(FP4X4),
-                lhsT_scale=w1s_dealt[:, P * t : P * (t + 1)],
-                rhs=picked_w[:].bitcast(FP8X4),
-                rhs_scale=picked_s[:],
-                start=True,
-                stop=True,
-            )
-            st = keep.tile([P, V + S], F32, name="sum_tab%d" % t)
-            dt_ = keep.tile([P, V + S], F32, name="dif_tab%d" % t)
-            nc.scalar.activation(st[:, V:], y[:], ACT.Copy)
-            nc.vector.tensor_tensor(dt_[:, V:], y[:], gains[t][:], ALU.mult)
-            nc.vector.tensor_tensor(st[:, :V], st[:, V :: 2], st[:, V + 1 :: 2], ALU.add)
-            nc.vector.tensor_tensor(dt_[:, :V], dt_[:, V :: 2], dt_[:, V + 1 :: 2], ALU.add)
-            sum_tab.append(st)
-            dif_tab.append(dt_)
+            wt = keep.tile([P, V + 2 * S], F32, name="w_tab%d" % t)
+            bt = keep.tile([P, V + S], F32, name="b_tab%d" % t)
+            nc.scalar.activation(wt[:, V + S :], gains[t][:], ACT.Identity, scale=sign_u[:, t : t + 1], bias=1.0)
+            w_tab.append(wt)
+            b_tab.append(bt)
+
+        def tables(t):
+            wt, bt = w_tab[t], b_tab[t]
+            spans = [(0, HALF), (HALF, S)] if t == 0 else [(0, S)]
+            for j0, j1 in spans:
+                y = psum.tile([P, j1 - j0], F32, name="y%d_%d" % (t, j0))
+                nc.tensor.matmul_mx(
+                    out=y[:],
+                    lhsT=w1w_dealt[:, 2 * P * t : 2 * P * (t + 1)].bitcast(FP4X4),
+                    lhsT_scale=w1s_dealt[:, P * t : P * (t + 1)],
+                    rhs=picked_w[:, j0:j1].bitcast(FP8X4),
+                    rhs_scale=picked_s[:, j0:j1],
+                    start=True,
+                    stop=True,
+                )
+                nc.vector.scalar_tensor_tensor(
+                    bt[:, V + j0 : V + j1], gains[t][:, j0:j1], sign_u[:, t : t + 1], y[:], ALU.subtract, ALU.mult
+                )
+                nc.vector.tensor_tensor(wt[:, V + j0 : V + j1], y[:], wt[:, V + S + j0 : V + S + j1], ALU.mult)
+            adder = nc.vector if t < 4 else nc.gpsimd
+            adder.tensor_tensor(bt[:, :V], bt[:, V : V + S : 2], bt[:, V + 1 : V + S : 2], ALU.add)
+            adder.tensor_tensor(wt[:, :V], wt[:, V : V + S : 2], wt[:, V + 1 : V + S : 2], ALU.add)
 
         steps = [(c, t) for c in range(len(CHUNKS)) for t in range(PACK)]
-        rot, mag, hid = {}, {}, {}
+        first, rot, sq = {}, {}, {}
 
         def lists(c):
             j0, w = CHUNKS[c]
             return ra_t[:, j0 // 16 : (j0 + w) // 16], rb_t[:, j0 // 16 : (j0 + w) // 16]
 
-        def fetch(c, t):
+        def fetch_a(c, t):
             w = CHUNKS[c][1]
             a, b = lists(c)
-            first = keep.tile([P, 2, w], F32, name="first%d_%d" % (c, t))
-            nc.scalar.activation(first[:, 0, :], sum_tab[t][:].indirect(a), ACT.Copy)
-            nc.scalar.activation(first[:, 1, :], dif_tab[t][:].indirect(a), ACT.Copy)
+            f = keep.tile([P, 2, w], F32, name="first%d_%d" % (c, t))
+            nc.scalar.activation(f[:, 0, :], b_tab[t][:].indirect(a), ACT.Copy)
+            nc.scalar.activation(f[:, 1, :], w_tab[t][:].indirect(a), ACT.Copy)
+            first[c, t] = f
+
+        def fetch_b(c, t):
+            w = CHUNKS[c][1]
+            a, b = lists(c)
+            f = first[c, t]
             r = keep.tile([P, 2, w], F32, name="rot%d_%d" % (c, t))
-            nc.vector.tensor_tensor(r[:, 0, :], dif_tab[t][:].indirect(b), first[:, 0, :], ALU.add)
-            nc.vector.tensor_tensor(r[:, 1, :], sum_tab[t][:].indirect(b), first[:, 1, :], ALU.subtract)
+            nc.vector.tensor_tensor(r[:, 0, :], w_tab[t][:].indirect(b), f[:, 0, :], ALU.subtract)
+            nc.vector.tensor_tensor(r[:, 1, :], b_tab[t][:].indirect(b), f[:, 1, :], ALU.add)
             rot[c, t] = r
 
-        def combine(c, t):
+        def squares(c, t):
             w = CHUNKS[c][1]
-            r = rot[c, t]
             a = keep.tile([P, 2, w], F32, name="abs%d_%d" % (c, t))
-            nc.scalar.activation(a[:], r[:], ACT.Abs)
-            prod = keep.tile([P, w], F32, name="prod%d_%d" % (c, t))
-            nc.vector.scalar_tensor_tensor(prod[:], r[:, 0, :], u[:, t : t + 1], r[:, 1, :], ALU.mult, ALU.mult)
-            m = keep.tile([P, w], F32, name="max%d_%d" % (c, t))
-            nc.vector.tensor_tensor(m[:], a[:, 0, :], a[:, 1, :], ALU.max)
             if t == 0:
-                hid[c] = keep.tile([P, PACK, w], BF16, name="hid%d" % c)
-            nc.vector.scalar_tensor_tensor(hid[c][:, t, :], m[:], neg_u[:, t : t + 1], prod[:], ALU.mult, ALU.add)
+                sq[c] = [keep.tile([P, PACK, w], F32, name="sq%d_%d" % (c, i)) for i in range(2)]
+            if (c, t) in ON_VECTOR:
+                nc.scalar.activation(a[:], rot[c, t][:], ACT.Abs, scale=half_root[:, t : t + 1])
+                for i, shift in enumerate((shift_x, shift_y)):
+                    nc.vector.scalar_tensor_tensor(
+                        sq[c][i][:, t, :], a[:, i, :], shift[:, t : t + 1], a[:, i, :], ALU.add, ALU.mult
+                    )
+            else:
+                nc.scalar.activation(a[:], rot[c, t][:], ACT.Abs)
+                for i, bias in enumerate((bias_x, bias_y)):
+                    nc.scalar.activation(
+                        sq[c][i][:, t, :], a[:, i, :], ACT.Square, scale=half_root[:, t : t + 1], bias=bias[:, t : t + 1]
+                    )
 
         def finish(c):
             j0, w = CHUNKS[c]
             woven = keep.tile([P, w, PACK], BF16, name="woven%d" % c, align_bytes=64)
-            nc.scalar.copy(
-                out=woven[:].rearrange("p (c i) t -> p c t i", i=4),
-                in_=hid[c][:].rearrange("p t (c i) -> p c t i", i=4),
+            nc.vector.tensor_tensor(
+                woven[:].rearrange("p (c i) t -> p c t i", i=4),
+                sq[c][0][:].rearrange("p t (c i) -> p c t i", i=4),
+                sq[c][1][:].rearrange("p t (c i) -> p c t i", i=4),
+                ALU.subtract,
             )
             codes = keep.tile([P, w], U32, name="codes%d" % c, align_bytes=64)
             scales = keep.tile([P, w], U8, name="scales%d" % c, align_bytes=64)
@@ -147,23 +196,34 @@ def tile_picked_yrotqv_mul_p_kernel(
                 out=codes[:].bitcast(FP8X4), scales=scales[:], in_=woven[:].rearrange("p w t -> p (w t)")
             )
             acc = psum.tile([P, w], F32, name="acc%d" % c)
-            nc.tensor.matmul_mx(
-                out=acc[:],
-                lhsT=w2w[:].bitcast(FP4X4),
-                lhsT_scale=w2s[:],
-                rhs=codes[:].bitcast(FP8X4),
-                rhs_scale=scales[:],
-                start=True,
-                stop=True,
-            )
+            for n0 in range(0, w, 256):
+                n1 = min(w, n0 + 256)
+                nc.tensor.matmul_mx(
+                    out=acc[:, n0:n1],
+                    lhsT=w2w[:].bitcast(FP4X4),
+                    lhsT_scale=w2s[:],
+                    rhs=codes[:, n0:n1].bitcast(FP8X4),
+                    rhs_scale=scales[:, n0:n1],
+                    start=True,
+                    stop=True,
+                )
             res = keep.tile([P, w], F32, name="res%d" % c)
-            nc.scalar.activation(res[:], acc[:], ACT.Copy)
+            if c + 1 < len(CHUNKS):
+                nc.scalar.copy(res[:], acc[:])
+            else:
+                nc.vector.tensor_copy(res[:], acc[:])
             nc.sync.dma_start(out=out[:, j0 : j0 + w], in_=res[:])
 
-        for i in range(len(steps) + 2):
+        tables(0)
+        for i in range(len(steps) + 3):
+            if i + 1 < PACK:
+                tables(i + 1)
             if i < len(steps):
-                fetch(*steps[i])
+                fetch_a(*steps[i])
             if 1 <= i <= len(steps):
-                combine(*steps[i - 1])
-            if i >= 2 and steps[i - 2][1] == PACK - 1:
-                finish(steps[i - 2][0])
+                squares_step = steps[i - 1]
+                fetch_b(*squares_step)
+            if 2 <= i <= len(steps) + 1:
+                squares(*steps[i - 2])
+            if i >= 3 and steps[i - 3][1] == PACK - 1:
+                finish(steps[i - 3][0])

@@ -19,8 +19,8 @@ ACT = mybir.ActivationFunctionType
 P = 128
 PACK = 4
 CHUNKS = [(0, 384), (384, 128)]
-TINY = 1e-30
-ON_VECTOR = [(0, 0)]
+CUT = (2, 3)
+ON_VECTOR = [(0, 1), (0, 3)]
 
 
 def load_scale_rows(queue, plane, rows):
@@ -55,37 +55,35 @@ def tile_picked_yrotqv_mul_p_kernel(
 
         nc.sync.dma_start(out=w1w[:].bitcast(I32), in_=w1_words[0].bitcast(I32))
         nc.sync.dma_start(offs_t[:], offs)
+        nc.sync.dma_start(out=u[:], in_=unit.rearrange("(p t) o -> p (t o)", t=PACK))
         load_scale_rows(nc.sync, xs, x_scales[0])
         nc.sync.dma_start(out=xw[:].bitcast(I32), in_=x_words[0].rearrange("p n t -> p (n t)").bitcast(I32))
         load_scale_rows(nc.sync, w1s, w1_scales[0])
-        nc.sync.dma_start(out=u[:], in_=unit.rearrange("(p t) o -> p (t o)", t=PACK))
         sg_rows = sg.rearrange("(p t) j -> p t j", t=PACK)
-        for t in range(PACK):
+        for t in range(PACK - 1):
             nc.sync.dma_start(out=gains[t][:], in_=sg_rows[:, t, :])
         nc.sync.dma_start(ra_t[:], ra)
         nc.sync.dma_start(rb_t[:], rb)
+        nc.sync.dma_start(out=gains[PACK - 1][:], in_=sg_rows[:, PACK - 1, :])
         nc.sync.dma_start(out=w2w[:].bitcast(I32), in_=w2_words[0].bitcast(I32))
         load_scale_rows(nc.sync, w2s, w2_scales[0])
 
-        mag_u = keep.tile([P, PACK], F32, name="mag_u")
-        root0 = keep.tile([P, PACK], F32, name="root0")
         sign_u = keep.tile([P, PACK], F32, name="sign_u")
-        inv = keep.tile([P, PACK], F32, name="inv")
-        quot = keep.tile([P, PACK], F32, name="quot")
+        quarter_mag = keep.tile([P, PACK], F32, name="quarter_mag")
+        exponent = keep.tile([P, PACK], F32, name="exponent")
         half_root = keep.tile([P, PACK], F32, name="half_root")
         bias_x = keep.tile([P, PACK], F32, name="bias_x")
         bias_y = keep.tile([P, PACK], F32, name="bias_y")
-        nc.gpsimd.tensor_scalar(mag_u[:], u[:], 0.0, 2.0, ALU.is_ge, ALU.mult)
-        nc.gpsimd.tensor_scalar(sign_u[:], mag_u[:], 1.0, -1.0, ALU.mult, ALU.add)
-        nc.gpsimd.tensor_tensor(mag_u[:], u[:], sign_u[:], ALU.mult)
-        nc.scalar.activation(root0[:], mag_u[:], ACT.Sqrt)
-        nc.gpsimd.tensor_scalar(inv[:], root0[:], TINY, None, ALU.max)
-        nc.vector.reciprocal(inv[:], inv[:])
-        nc.gpsimd.tensor_tensor(quot[:], mag_u[:], inv[:], ALU.mult)
-        nc.gpsimd.tensor_tensor(quot[:], quot[:], root0[:], ALU.add)
-        nc.gpsimd.tensor_scalar(half_root[:], quot[:], 0.25, None, ALU.mult)
+        shift_x = keep.tile([P, PACK], F32, name="shift_x")
+        shift_y = keep.tile([P, PACK], F32, name="shift_y")
+        nc.gpsimd.memset(exponent[:], 0.5)
+        nc.scalar.activation(sign_u[:], u[:], ACT.Sign)
+        nc.scalar.activation(quarter_mag[:], u[:], ACT.Abs, scale=0.25)
+        nc.gpsimd.tensor_tensor(half_root[:], quarter_mag[:], exponent[:], ALU.pow)
         nc.gpsimd.tensor_tensor(bias_y[:], half_root[:], sign_u[:], ALU.mult)
-        nc.gpsimd.tensor_scalar(bias_x[:], bias_y[:], -1.0, None, ALU.mult)
+        nc.scalar.activation(bias_x[:], bias_y[:], ACT.Copy, scale=-1.0)
+        nc.scalar.activation(shift_x[:], bias_y[:], ACT.Copy, scale=-2.0)
+        nc.scalar.activation(shift_y[:], bias_y[:], ACT.Copy, scale=2.0)
 
         w1w_dealt = keep.tile([P, 2 * H], U8, name="w1w_dealt", align_bytes=64)
         w1s_dealt = keep.tile([P, H], U8, name="w1s_dealt", align_bytes=64)
@@ -103,11 +101,6 @@ def tile_picked_yrotqv_mul_p_kernel(
         nc.vector.tensor_copy(out=dealt_view[:, 0, :], in_=raw_view[:, 0, :])
         nc.vector.tensor_copy(picked_w[:, HALF:], xw[:].indirect(offs_t[:, HALF // 16 :]))
         nc.vector.tensor_copy(out=dealt_view[:, 1:, :], in_=raw_view[:, 1:, :])
-
-        shift_x = keep.tile([P, PACK], F32, name="shift_x")
-        shift_y = keep.tile([P, PACK], F32, name="shift_y")
-        nc.gpsimd.tensor_scalar(shift_y[:], bias_y[:], 2.0, None, ALU.mult)
-        nc.gpsimd.tensor_scalar(shift_x[:], bias_y[:], -2.0, None, ALU.mult)
 
         w_tab, b_tab = [], []
         for t in range(PACK):
@@ -135,50 +128,46 @@ def tile_picked_yrotqv_mul_p_kernel(
                     bt[:, V + j0 : V + j1], gains[t][:, j0:j1], sign_u[:, t : t + 1], y[:], ALU.subtract, ALU.mult
                 )
                 nc.vector.tensor_tensor(wt[:, V + j0 : V + j1], y[:], wt[:, V + S + j0 : V + S + j1], ALU.mult)
-            adder = nc.vector if t < 4 else nc.gpsimd
+            adder = nc.gpsimd if t in (1, 2) else nc.vector
             adder.tensor_tensor(bt[:, :V], bt[:, V : V + S : 2], bt[:, V + 1 : V + S : 2], ALU.add)
             adder.tensor_tensor(wt[:, :V], wt[:, V : V + S : 2], wt[:, V + 1 : V + S : 2], ALU.add)
 
-        steps = [(c, t) for c in range(len(CHUNKS)) for t in range(PACK)]
-        first, rot, sq = {}, {}, {}
+        steps = [(c, t) for c in range(len(CHUNKS)) for t in range(PACK) if c == 0 or t in CUT]
+        first = [keep.tile([P, 2, S], F32, name="first%d" % t) for t in range(PACK)]
+        sq = [keep.tile([P, PACK, S], F32, name="sq%d" % i) for i in range(2)]
+        rot = {}
 
-        def lists(c):
-            j0, w = CHUNKS[c]
-            return ra_t[:, j0 // 16 : (j0 + w) // 16], rb_t[:, j0 // 16 : (j0 + w) // 16]
+        def span(c, t):
+            return CHUNKS[c] if t in CUT else (0, S)
 
         def fetch_a(c, t):
-            w = CHUNKS[c][1]
-            a, b = lists(c)
-            f = keep.tile([P, 2, w], F32, name="first%d_%d" % (c, t))
-            nc.scalar.activation(f[:, 0, :], b_tab[t][:].indirect(a), ACT.Copy)
-            nc.scalar.activation(f[:, 1, :], w_tab[t][:].indirect(a), ACT.Copy)
-            first[c, t] = f
+            if c == 0:
+                nc.scalar.activation(first[t][:, 0, :], b_tab[t][:].indirect(ra_t[:]), ACT.Copy)
+                nc.scalar.activation(first[t][:, 1, :], w_tab[t][:].indirect(ra_t[:]), ACT.Copy)
 
         def fetch_b(c, t):
-            w = CHUNKS[c][1]
-            a, b = lists(c)
-            f = first[c, t]
+            j0, w = span(c, t)
+            b = rb_t[:, j0 // 16 : (j0 + w) // 16]
+            f = first[t]
             r = keep.tile([P, 2, w], F32, name="rot%d_%d" % (c, t))
-            nc.vector.tensor_tensor(r[:, 0, :], w_tab[t][:].indirect(b), f[:, 0, :], ALU.subtract)
-            nc.vector.tensor_tensor(r[:, 1, :], b_tab[t][:].indirect(b), f[:, 1, :], ALU.add)
+            nc.vector.tensor_tensor(r[:, 0, :], w_tab[t][:].indirect(b), f[:, 0, j0 : j0 + w], ALU.subtract)
+            nc.vector.tensor_tensor(r[:, 1, :], b_tab[t][:].indirect(b), f[:, 1, j0 : j0 + w], ALU.add)
             rot[c, t] = r
 
         def squares(c, t):
-            w = CHUNKS[c][1]
+            j0, w = span(c, t)
             a = keep.tile([P, 2, w], F32, name="abs%d_%d" % (c, t))
-            if t == 0:
-                sq[c] = [keep.tile([P, PACK, w], F32, name="sq%d_%d" % (c, i)) for i in range(2)]
             if (c, t) in ON_VECTOR:
                 nc.scalar.activation(a[:], rot[c, t][:], ACT.Abs, scale=half_root[:, t : t + 1])
                 for i, shift in enumerate((shift_x, shift_y)):
                     nc.vector.scalar_tensor_tensor(
-                        sq[c][i][:, t, :], a[:, i, :], shift[:, t : t + 1], a[:, i, :], ALU.add, ALU.mult
+                        sq[i][:, t, j0 : j0 + w], a[:, i, :], shift[:, t : t + 1], a[:, i, :], ALU.add, ALU.mult
                     )
             else:
                 nc.scalar.activation(a[:], rot[c, t][:], ACT.Abs)
                 for i, bias in enumerate((bias_x, bias_y)):
                     nc.scalar.activation(
-                        sq[c][i][:, t, :], a[:, i, :], ACT.Square, scale=half_root[:, t : t + 1], bias=bias[:, t : t + 1]
+                        sq[i][:, t, j0 : j0 + w], a[:, i, :], ACT.Square, scale=half_root[:, t : t + 1], bias=bias[:, t : t + 1]
                     )
 
         def finish(c):
@@ -186,8 +175,8 @@ def tile_picked_yrotqv_mul_p_kernel(
             woven = keep.tile([P, w, PACK], BF16, name="woven%d" % c, align_bytes=64)
             nc.vector.tensor_tensor(
                 woven[:].rearrange("p (c i) t -> p c t i", i=4),
-                sq[c][0][:].rearrange("p t (c i) -> p c t i", i=4),
-                sq[c][1][:].rearrange("p t (c i) -> p c t i", i=4),
+                sq[0][:, :, j0 : j0 + w].rearrange("p t (c i) -> p c t i", i=4),
+                sq[1][:, :, j0 : j0 + w].rearrange("p t (c i) -> p c t i", i=4),
                 ALU.subtract,
             )
             codes = keep.tile([P, w], U32, name="codes%d" % c, align_bytes=64)
@@ -214,10 +203,11 @@ def tile_picked_yrotqv_mul_p_kernel(
                 nc.vector.tensor_copy(res[:], acc[:])
             nc.sync.dma_start(out=out[:, j0 : j0 + w], in_=res[:])
 
-        tables(0)
+        for t in range(4):
+            tables(t)
         for i in range(len(steps) + 3):
-            if i + 1 < PACK:
-                tables(i + 1)
+            if i + 4 < PACK:
+                tables(i + 4)
             if i < len(steps):
                 fetch_a(*steps[i])
             if 1 <= i <= len(steps):

@@ -18,14 +18,17 @@ ACT = mybir.ActivationFunctionType
 
 P = 128
 PACK = 4
+LIST_ROWS = 16
+HALF = S // 2
 CHUNKS = [(0, 384), (384, 128)]
-CUT = (2, 3)
-ON_VECTOR = [(0, 1), (0, 3)]
+FIRST_CUT_TILE = 2
+MAX_PASS = 256
+WEAVE = 4
 
 
-def load_scale_rows(queue, plane, rows):
+def load_scale_rows(nc, plane, rows):
     for q in range(4):
-        queue.dma_start(out=plane[32 * q : 32 * q + 4, :].bitcast(I32), in_=rows[4 * q : 4 * q + 4, :].bitcast(I32))
+        nc.sync.dma_start(out=plane[32 * q : 32 * q + 4, :].bitcast(I32), in_=rows[4 * q : 4 * q + 4, :].bitcast(I32))
 
 
 def tile_picked_yrotqv_mul_p_kernel(
@@ -36,16 +39,16 @@ def tile_picked_yrotqv_mul_p_kernel(
         keep = ctx.enter_context(tc.tile_pool(name="keep", bufs=1))
         psum = ctx.enter_context(tc.psum_pool(name="psum", bufs=1))
 
-        offs_t = keep.tile([P, S // 16], U16, name="offs_t")
-        ra_t = keep.tile([P, S // 16], U16, name="ra_t")
-        rb_t = keep.tile([P, S // 16], U16, name="rb_t")
+        offs_t = keep.tile([P, S // LIST_ROWS], U16, name="offs_t")
+        ra_t = keep.tile([P, S // LIST_ROWS], U16, name="ra_t")
+        rb_t = keep.tile([P, S // LIST_ROWS], U16, name="rb_t")
         xw = keep.tile([P, T], U32, name="xw", align_bytes=64)
         xs = keep.tile([P, T], U8, name="xs", align_bytes=64)
         w1w = keep.tile([P, 2 * H], U8, name="w1w", align_bytes=64)
         w1s = keep.tile([P, H], U8, name="w1s", align_bytes=64)
         w2w = keep.tile([P, 2 * N], U8, name="w2w", align_bytes=64)
         w2s = keep.tile([P, N], U8, name="w2s", align_bytes=64)
-        gains = [keep.tile([P, S], F32, name="gain%d" % t) for t in range(PACK)]
+        gains = keep.tile([P, PACK, S], F32, name="gains")
         u = keep.tile([P, PACK], F32, name="u")
 
         nc.vector.memset(xs[:, : T // 2].bitcast(I32), 0)
@@ -56,17 +59,16 @@ def tile_picked_yrotqv_mul_p_kernel(
         nc.sync.dma_start(out=w1w[:].bitcast(I32), in_=w1_words[0].bitcast(I32))
         nc.sync.dma_start(offs_t[:], offs)
         nc.sync.dma_start(out=u[:], in_=unit.rearrange("(p t) o -> p (t o)", t=PACK))
-        load_scale_rows(nc.sync, xs, x_scales[0])
+        load_scale_rows(nc, xs, x_scales[0])
         nc.sync.dma_start(out=xw[:].bitcast(I32), in_=x_words[0].rearrange("p n t -> p (n t)").bitcast(I32))
-        load_scale_rows(nc.sync, w1s, w1_scales[0])
+        load_scale_rows(nc, w1s, w1_scales[0])
         sg_rows = sg.rearrange("(p t) j -> p t j", t=PACK)
-        for t in range(PACK - 1):
-            nc.sync.dma_start(out=gains[t][:], in_=sg_rows[:, t, :])
+        for t0, t1 in ((0, 1), (1, 2), (2, PACK)):
+            nc.sync.dma_start(out=gains[:, t0:t1, :], in_=sg_rows[:, t0:t1, :])
         nc.sync.dma_start(ra_t[:], ra)
         nc.sync.dma_start(rb_t[:], rb)
-        nc.sync.dma_start(out=gains[PACK - 1][:], in_=sg_rows[:, PACK - 1, :])
         nc.sync.dma_start(out=w2w[:].bitcast(I32), in_=w2_words[0].bitcast(I32))
-        load_scale_rows(nc.sync, w2s, w2_scales[0])
+        load_scale_rows(nc, w2s, w2_scales[0])
 
         sign_u = keep.tile([P, PACK], F32, name="sign_u")
         quarter_mag = keep.tile([P, PACK], F32, name="quarter_mag")
@@ -94,25 +96,28 @@ def tile_picked_yrotqv_mul_p_kernel(
         picked_s = keep.tile([P, S], U8, name="picked_s", align_bytes=64)
         picked_w = keep.tile([P, S], U32, name="picked_w", align_bytes=64)
         nc.vector.tensor_copy(picked_s[:], xs[:].indirect(offs_t[:]))
-        dealt_view = w1s_dealt[:].rearrange("p (t m) -> p t m", t=PACK)
-        raw_view = w1s[:].rearrange("p (m t) -> p t m", t=PACK)
-        HALF = S // 2
-        nc.vector.tensor_copy(picked_w[:, :HALF], xw[:].indirect(offs_t[:, : HALF // 16]))
-        nc.vector.tensor_copy(out=dealt_view[:, 0, :], in_=raw_view[:, 0, :])
-        nc.vector.tensor_copy(picked_w[:, HALF:], xw[:].indirect(offs_t[:, HALF // 16 :]))
-        nc.vector.tensor_copy(out=dealt_view[:, 1:, :], in_=raw_view[:, 1:, :])
+        w1s_by_tile = w1s[:].rearrange("p (m t) -> p t m", t=PACK)
+        w1s_dealt_by_tile = w1s_dealt[:].rearrange("p (t m) -> p t m", t=PACK)
+        nc.vector.tensor_copy(picked_w[:, :HALF], xw[:].indirect(offs_t[:, : HALF // LIST_ROWS]))
+        nc.gpsimd.tensor_copy(out=w1s_dealt_by_tile[:, 0, :], in_=w1s_by_tile[:, 0, :])
+        nc.vector.tensor_copy(picked_w[:, HALF:], xw[:].indirect(offs_t[:, HALF // LIST_ROWS :]))
+        nc.gpsimd.tensor_copy(out=w1s_dealt_by_tile[:, 1:, :], in_=w1s_by_tile[:, 1:, :])
 
-        w_tab, b_tab = [], []
+        plus_tiles, minus_tiles = [], []
         for t in range(PACK):
-            wt = keep.tile([P, V + 2 * S], F32, name="w_tab%d" % t)
-            bt = keep.tile([P, V + S], F32, name="b_tab%d" % t)
-            nc.scalar.activation(wt[:, V + S :], gains[t][:], ACT.Identity, scale=sign_u[:, t : t + 1], bias=1.0)
-            w_tab.append(wt)
-            b_tab.append(bt)
+            plus = keep.tile([P, V + 2 * S], F32, name="plus%d" % t)
+            minus = keep.tile([P, V + S], F32, name="minus%d" % t)
+            nc.scalar.activation(plus[:, V + S :], gains[:, t, :], ACT.Identity, scale=sign_u[:, t : t + 1], bias=1.0)
+            plus_tiles.append(plus)
+            minus_tiles.append(minus)
 
-        def tables(t):
-            wt, bt = w_tab[t], b_tab[t]
+        def pair_sums(engine, tab):
+            engine.tensor_tensor(tab[:, :V], tab[:, V : V + S : 2], tab[:, V + 1 : V + S : 2], ALU.add)
+
+        def make_tables(t):
+            plus, minus = plus_tiles[t], minus_tiles[t]
             spans = [(0, HALF), (HALF, S)] if t == 0 else [(0, S)]
+            banks = []
             for j0, j1 in spans:
                 y = psum.tile([P, j1 - j0], F32, name="y%d_%d" % (t, j0))
                 nc.tensor.matmul_mx(
@@ -125,68 +130,73 @@ def tile_picked_yrotqv_mul_p_kernel(
                     stop=True,
                 )
                 nc.vector.scalar_tensor_tensor(
-                    bt[:, V + j0 : V + j1], gains[t][:, j0:j1], sign_u[:, t : t + 1], y[:], ALU.subtract, ALU.mult
+                    minus[:, V + j0 : V + j1], gains[:, t, j0:j1], sign_u[:, t : t + 1], y[:], ALU.subtract, ALU.mult
                 )
-                nc.vector.tensor_tensor(wt[:, V + j0 : V + j1], y[:], wt[:, V + S + j0 : V + S + j1], ALU.mult)
-            adder = nc.gpsimd if t in (1, 2) else nc.vector
-            adder.tensor_tensor(bt[:, :V], bt[:, V : V + S : 2], bt[:, V + 1 : V + S : 2], ALU.add)
-            adder.tensor_tensor(wt[:, :V], wt[:, V : V + S : 2], wt[:, V + 1 : V + S : 2], ALU.add)
+                banks.append(y)
+            last = t == PACK - 1
+            pair_sums(nc.vector if t == 0 or last else nc.gpsimd, minus)
+            for (j0, j1), y in zip(spans, banks):
+                nc.vector.tensor_tensor(plus[:, V + j0 : V + j1], y[:], plus[:, V + S + j0 : V + S + j1], ALU.mult)
+            pair_sums(nc.vector if last else nc.gpsimd, plus)
 
-        steps = [(c, t) for c in range(len(CHUNKS)) for t in range(PACK) if c == 0 or t in CUT]
-        first = [keep.tile([P, 2, S], F32, name="first%d" % t) for t in range(PACK)]
-        sq = [keep.tile([P, PACK, S], F32, name="sq%d" % i) for i in range(2)]
-        rot = {}
+        steps = [(c, t) for c in range(len(CHUNKS)) for t in range(PACK) if c == 0 or t >= FIRST_CUT_TILE]
+        by_ra = [keep.tile([P, 2, S], F32, name="by_ra%d" % t) for t in range(PACK)]
+        squared = [keep.tile([P, PACK, S], F32, name="squared%d" % i) for i in range(2)]
+        xy = {}
 
-        def span(c, t):
-            return CHUNKS[c] if t in CUT else (0, S)
+        def columns(c, t):
+            return CHUNKS[c] if t >= FIRST_CUT_TILE else (0, S)
 
-        def fetch_a(c, t):
-            if c == 0:
-                nc.scalar.activation(first[t][:, 0, :], b_tab[t][:].indirect(ra_t[:]), ACT.Copy)
-                nc.scalar.activation(first[t][:, 1, :], w_tab[t][:].indirect(ra_t[:]), ACT.Copy)
+        def look_up_ra(t):
+            nc.scalar.activation(by_ra[t][:, 0, :], minus_tiles[t][:].indirect(ra_t[:]), ACT.Copy)
+            nc.scalar.activation(by_ra[t][:, 1, :], plus_tiles[t][:].indirect(ra_t[:]), ACT.Copy)
 
-        def fetch_b(c, t):
-            j0, w = span(c, t)
-            b = rb_t[:, j0 // 16 : (j0 + w) // 16]
-            f = first[t]
-            r = keep.tile([P, 2, w], F32, name="rot%d_%d" % (c, t))
-            nc.vector.tensor_tensor(r[:, 0, :], w_tab[t][:].indirect(b), f[:, 0, j0 : j0 + w], ALU.subtract)
-            nc.vector.tensor_tensor(r[:, 1, :], b_tab[t][:].indirect(b), f[:, 1, j0 : j0 + w], ALU.add)
-            rot[c, t] = r
+        def look_up_rb(c, t):
+            j0, w = columns(c, t)
+            rb_part = rb_t[:, j0 // LIST_ROWS : (j0 + w) // LIST_ROWS]
+            pair = keep.tile([P, 2, w], F32, name="xy%d_%d" % (c, t))
+            nc.vector.tensor_tensor(
+                pair[:, 0, :], plus_tiles[t][:].indirect(rb_part), by_ra[t][:, 0, j0 : j0 + w], ALU.subtract
+            )
+            nc.vector.tensor_tensor(
+                pair[:, 1, :], minus_tiles[t][:].indirect(rb_part), by_ra[t][:, 1, j0 : j0 + w], ALU.add
+            )
+            xy[c, t] = pair
 
-        def squares(c, t):
-            j0, w = span(c, t)
-            a = keep.tile([P, 2, w], F32, name="abs%d_%d" % (c, t))
-            if (c, t) in ON_VECTOR:
-                nc.scalar.activation(a[:], rot[c, t][:], ACT.Abs, scale=half_root[:, t : t + 1])
+        def square(c, t):
+            j0, w = columns(c, t)
+            mags = keep.tile([P, 2, w], F32, name="mags%d_%d" % (c, t))
+            h = half_root[:, t : t + 1]
+            if t % 2 == 1:
+                nc.scalar.activation(mags[:], xy[c, t][:], ACT.Abs, scale=h)
                 for i, shift in enumerate((shift_x, shift_y)):
                     nc.vector.scalar_tensor_tensor(
-                        sq[i][:, t, j0 : j0 + w], a[:, i, :], shift[:, t : t + 1], a[:, i, :], ALU.add, ALU.mult
+                        squared[i][:, t, j0 : j0 + w], mags[:, i, :], shift[:, t : t + 1], mags[:, i, :], ALU.add, ALU.mult
                     )
             else:
-                nc.scalar.activation(a[:], rot[c, t][:], ACT.Abs)
+                nc.scalar.activation(mags[:], xy[c, t][:], ACT.Abs)
                 for i, bias in enumerate((bias_x, bias_y)):
                     nc.scalar.activation(
-                        sq[i][:, t, j0 : j0 + w], a[:, i, :], ACT.Square, scale=half_root[:, t : t + 1], bias=bias[:, t : t + 1]
+                        squared[i][:, t, j0 : j0 + w], mags[:, i, :], ACT.Square, scale=h, bias=bias[:, t : t + 1]
                     )
 
         def finish(c):
             j0, w = CHUNKS[c]
-            woven = keep.tile([P, w, PACK], BF16, name="woven%d" % c, align_bytes=64)
+            hid = keep.tile([P, w, PACK], BF16, name="hid%d" % c, align_bytes=64)
             nc.vector.tensor_tensor(
-                woven[:].rearrange("p (c i) t -> p c t i", i=4),
-                sq[0][:, :, j0 : j0 + w].rearrange("p t (c i) -> p c t i", i=4),
-                sq[1][:, :, j0 : j0 + w].rearrange("p t (c i) -> p c t i", i=4),
+                hid[:].rearrange("p (c i) t -> p c t i", i=WEAVE),
+                squared[0][:, :, j0 : j0 + w].rearrange("p t (c i) -> p c t i", i=WEAVE),
+                squared[1][:, :, j0 : j0 + w].rearrange("p t (c i) -> p c t i", i=WEAVE),
                 ALU.subtract,
             )
             codes = keep.tile([P, w], U32, name="codes%d" % c, align_bytes=64)
             scales = keep.tile([P, w], U8, name="scales%d" % c, align_bytes=64)
             nc.vector.quantize_mx(
-                out=codes[:].bitcast(FP8X4), scales=scales[:], in_=woven[:].rearrange("p w t -> p (w t)")
+                out=codes[:].bitcast(FP8X4), scales=scales[:], in_=hid[:].rearrange("p w t -> p (w t)")
             )
             acc = psum.tile([P, w], F32, name="acc%d" % c)
-            for n0 in range(0, w, 256):
-                n1 = min(w, n0 + 256)
+            for n0 in range(0, w, MAX_PASS):
+                n1 = min(w, n0 + MAX_PASS)
                 nc.tensor.matmul_mx(
                     out=acc[:, n0:n1],
                     lhsT=w2w[:].bitcast(FP4X4),
@@ -203,17 +213,14 @@ def tile_picked_yrotqv_mul_p_kernel(
                 nc.vector.tensor_copy(res[:], acc[:])
             nc.sync.dma_start(out=out[:, j0 : j0 + w], in_=res[:])
 
-        for t in range(4):
-            tables(t)
+        for t in range(PACK):
+            make_tables(t)
         for i in range(len(steps) + 3):
-            if i + 4 < PACK:
-                tables(i + 4)
-            if i < len(steps):
-                fetch_a(*steps[i])
-            if 1 <= i <= len(steps):
-                squares_step = steps[i - 1]
-                fetch_b(*squares_step)
-            if 2 <= i <= len(steps) + 1:
-                squares(*steps[i - 2])
+            if i < PACK:
+                look_up_ra(i)
+            if 0 <= i - 1 < len(steps):
+                look_up_rb(*steps[i - 1])
+            if 0 <= i - 2 < len(steps):
+                square(*steps[i - 2])
             if i >= 3 and steps[i - 3][1] == PACK - 1:
                 finish(steps[i - 3][0])

from contextlib import ExitStack

import concourse.mybir as mybir

K, T, S, N, H, V = 512, 2048, 512, 128, 512, 256
FLOPS = 2 * K * H * S + 2 * H * N * S

F32 = mybir.dt.float32
BF16 = mybir.dt.bfloat16
I32 = mybir.dt.int32
U32 = mybir.dt.uint32
U16 = mybir.dt.uint16
U8 = mybir.dt.uint8
FP8X4 = mybir.dt.float8_e4m3fn_x4
FP4X4 = mybir.dt.float4_e2m1fn_x4
ALU = mybir.AluOpType
ACT = mybir.ActivationFunctionType

P = 128
PACK = 4
LIST_ROWS = 16
HALF = S // 2
CHUNKS = [(0, 384), (384, 128)]
FIRST_CUT_TILE = 2
MAX_PASS = 256
WEAVE = 4


def load_scale_rows(nc, plane, rows):
    for q in range(4):
        nc.sync.dma_start(out=plane[32 * q : 32 * q + 4, :].bitcast(I32), in_=rows[4 * q : 4 * q + 4, :].bitcast(I32))


def tile_picked_yrotqv_mul_p_kernel(
    tc, x_words, x_scales, w1_words, w1_scales, sg, unit, w2_words, w2_scales, offs, ra, rb, out
):
    nc = tc.nc
    with ExitStack() as ctx:
        keep = ctx.enter_context(tc.tile_pool(name="keep", bufs=1))
        psum = ctx.enter_context(tc.psum_pool(name="psum", bufs=1))

        offs_t = keep.tile([P, S // LIST_ROWS], U16, name="offs_t")
        ra_t = keep.tile([P, S // LIST_ROWS], U16, name="ra_t")
        rb_t = keep.tile([P, S // LIST_ROWS], U16, name="rb_t")
        xw = keep.tile([P, T], U32, name="xw", align_bytes=64)
        xs = keep.tile([P, T], U8, name="xs", align_bytes=64)
        w1w = keep.tile([P, 2 * H], U8, name="w1w", align_bytes=64)
        w1s = keep.tile([P, H], U8, name="w1s", align_bytes=64)
        w2w = keep.tile([P, 2 * N], U8, name="w2w", align_bytes=64)
        w2s = keep.tile([P, N], U8, name="w2s", align_bytes=64)
        gains = keep.tile([P, PACK, S], F32, name="gains")
        u = keep.tile([P, PACK], F32, name="u")

        nc.vector.memset(xs[:, : T // 2].bitcast(I32), 0)
        nc.gpsimd.memset(xs[:, T // 2 :].bitcast(I32), 0)
        nc.vector.memset(w1s[:].bitcast(I32), 0)
        nc.gpsimd.memset(w2s[:].bitcast(I32), 0)

        nc.sync.dma_start(out=w1w[:].bitcast(I32), in_=w1_words[0].bitcast(I32))
        nc.sync.dma_start(offs_t[:], offs)
        nc.sync.dma_start(out=u[:], in_=unit.rearrange("(p t) o -> p (t o)", t=PACK))
        load_scale_rows(nc, xs, x_scales[0])
        nc.sync.dma_start(out=xw[:].bitcast(I32), in_=x_words[0].rearrange("p n t -> p (n t)").bitcast(I32))
        load_scale_rows(nc, w1s, w1_scales[0])
        sg_rows = sg.rearrange("(p t) j -> p t j", t=PACK)
        for t0, t1 in ((0, 1), (1, 2), (2, PACK)):
            nc.sync.dma_start(out=gains[:, t0:t1, :], in_=sg_rows[:, t0:t1, :])
        nc.sync.dma_start(ra_t[:], ra)
        nc.sync.dma_start(rb_t[:], rb)
        nc.sync.dma_start(out=w2w[:].bitcast(I32), in_=w2_words[0].bitcast(I32))
        load_scale_rows(nc, w2s, w2_scales[0])

        sign_u = keep.tile([P, PACK], F32, name="sign_u")
        quarter_mag = keep.tile([P, PACK], F32, name="quarter_mag")
        exponent = keep.tile([P, PACK], F32, name="exponent")
        half_root = keep.tile([P, PACK], F32, name="half_root")
        bias_x = keep.tile([P, PACK], F32, name="bias_x")
        bias_y = keep.tile([P, PACK], F32, name="bias_y")
        shift_x = keep.tile([P, PACK], F32, name="shift_x")
        shift_y = keep.tile([P, PACK], F32, name="shift_y")
        nc.gpsimd.memset(exponent[:], 0.5)
        nc.scalar.activation(sign_u[:], u[:], ACT.Sign)
        nc.scalar.activation(quarter_mag[:], u[:], ACT.Abs, scale=0.25)
        nc.gpsimd.tensor_tensor(half_root[:], quarter_mag[:], exponent[:], ALU.pow)
        nc.gpsimd.tensor_tensor(bias_y[:], half_root[:], sign_u[:], ALU.mult)
        nc.scalar.activation(bias_x[:], bias_y[:], ACT.Copy, scale=-1.0)
        nc.scalar.activation(shift_x[:], bias_y[:], ACT.Copy, scale=-2.0)
        nc.scalar.activation(shift_y[:], bias_y[:], ACT.Copy, scale=2.0)

        w1w_dealt = keep.tile([P, 2 * H], U8, name="w1w_dealt", align_bytes=64)
        w1s_dealt = keep.tile([P, H], U8, name="w1s_dealt", align_bytes=64)
        nc.vector.tensor_copy(
            out=w1w_dealt[:].rearrange("p (t m b) -> p t m b", t=PACK, b=2),
            in_=w1w[:].rearrange("p (m t b) -> p t m b", t=PACK, b=2),
        )
        picked_s = keep.tile([P, S], U8, name="picked_s", align_bytes=64)
        picked_w = keep.tile([P, S], U32, name="picked_w", align_bytes=64)
        nc.vector.tensor_copy(picked_s[:], xs[:].indirect(offs_t[:]))
        w1s_by_tile = w1s[:].rearrange("p (m t) -> p t m", t=PACK)
        w1s_dealt_by_tile = w1s_dealt[:].rearrange("p (t m) -> p t m", t=PACK)
        nc.vector.tensor_copy(picked_w[:, :HALF], xw[:].indirect(offs_t[:, : HALF // LIST_ROWS]))
        nc.gpsimd.tensor_copy(out=w1s_dealt_by_tile[:, 0, :], in_=w1s_by_tile[:, 0, :])
        nc.vector.tensor_copy(picked_w[:, HALF:], xw[:].indirect(offs_t[:, HALF // LIST_ROWS :]))
        nc.gpsimd.tensor_copy(out=w1s_dealt_by_tile[:, 1:, :], in_=w1s_by_tile[:, 1:, :])

        plus_tiles, minus_tiles = [], []
        for t in range(PACK):
            plus = keep.tile([P, V + 2 * S], F32, name="plus%d" % t)
            minus = keep.tile([P, V + S], F32, name="minus%d" % t)
            nc.scalar.activation(plus[:, V + S :], gains[:, t, :], ACT.Identity, scale=sign_u[:, t : t + 1], bias=1.0)
            plus_tiles.append(plus)
            minus_tiles.append(minus)

        def pair_sums(engine, tab):
            engine.tensor_tensor(tab[:, :V], tab[:, V : V + S : 2], tab[:, V + 1 : V + S : 2], ALU.add)

        def make_tables(t):
            plus, minus = plus_tiles[t], minus_tiles[t]
            spans = [(0, HALF), (HALF, S)] if t == 0 else [(0, S)]
            banks = []
            for j0, j1 in spans:
                y = psum.tile([P, j1 - j0], F32, name="y%d_%d" % (t, j0))
                nc.tensor.matmul_mx(
                    out=y[:],
                    lhsT=w1w_dealt[:, 2 * P * t : 2 * P * (t + 1)].bitcast(FP4X4),
                    lhsT_scale=w1s_dealt[:, P * t : P * (t + 1)],
                    rhs=picked_w[:, j0:j1].bitcast(FP8X4),
                    rhs_scale=picked_s[:, j0:j1],
                    start=True,
                    stop=True,
                )
                nc.vector.scalar_tensor_tensor(
                    minus[:, V + j0 : V + j1], gains[:, t, j0:j1], sign_u[:, t : t + 1], y[:], ALU.subtract, ALU.mult
                )
                banks.append(y)
            last = t == PACK - 1
            pair_sums(nc.vector if t == 0 or last else nc.gpsimd, minus)
            for (j0, j1), y in zip(spans, banks):
                nc.vector.tensor_tensor(plus[:, V + j0 : V + j1], y[:], plus[:, V + S + j0 : V + S + j1], ALU.mult)
            pair_sums(nc.vector if last else nc.gpsimd, plus)

        steps = [(c, t) for c in range(len(CHUNKS)) for t in range(PACK) if c == 0 or t >= FIRST_CUT_TILE]
        by_ra = [keep.tile([P, 2, S], F32, name="by_ra%d" % t) for t in range(PACK)]
        squared = [keep.tile([P, PACK, S], F32, name="squared%d" % i) for i in range(2)]
        xy = {}

        def columns(c, t):
            return CHUNKS[c] if t >= FIRST_CUT_TILE else (0, S)

        def look_up_ra(t):
            nc.scalar.activation(by_ra[t][:, 0, :], minus_tiles[t][:].indirect(ra_t[:]), ACT.Copy)
            nc.scalar.activation(by_ra[t][:, 1, :], plus_tiles[t][:].indirect(ra_t[:]), ACT.Copy)

        def look_up_rb(c, t):
            j0, w = columns(c, t)
            rb_part = rb_t[:, j0 // LIST_ROWS : (j0 + w) // LIST_ROWS]
            pair = keep.tile([P, 2, w], F32, name="xy%d_%d" % (c, t))
            nc.vector.tensor_tensor(
                pair[:, 0, :], plus_tiles[t][:].indirect(rb_part), by_ra[t][:, 0, j0 : j0 + w], ALU.subtract
            )
            nc.vector.tensor_tensor(
                pair[:, 1, :], minus_tiles[t][:].indirect(rb_part), by_ra[t][:, 1, j0 : j0 + w], ALU.add
            )
            xy[c, t] = pair

        def square(c, t):
            j0, w = columns(c, t)
            mags = keep.tile([P, 2, w], F32, name="mags%d_%d" % (c, t))
            h = half_root[:, t : t + 1]
            if t % 2 == 1:
                nc.scalar.activation(mags[:], xy[c, t][:], ACT.Abs, scale=h)
                for i, shift in enumerate((shift_x, shift_y)):
                    nc.vector.scalar_tensor_tensor(
                        squared[i][:, t, j0 : j0 + w], mags[:, i, :], shift[:, t : t + 1], mags[:, i, :], ALU.add, ALU.mult
                    )
            else:
                nc.scalar.activation(mags[:], xy[c, t][:], ACT.Abs)
                for i, bias in enumerate((bias_x, bias_y)):
                    nc.scalar.activation(
                        squared[i][:, t, j0 : j0 + w], mags[:, i, :], ACT.Square, scale=h, bias=bias[:, t : t + 1]
                    )

        def finish(c):
            j0, w = CHUNKS[c]
            hid = keep.tile([P, w, PACK], BF16, name="hid%d" % c, align_bytes=64)
            nc.vector.tensor_tensor(
                hid[:].rearrange("p (c i) t -> p c t i", i=WEAVE),
                squared[0][:, :, j0 : j0 + w].rearrange("p t (c i) -> p c t i", i=WEAVE),
                squared[1][:, :, j0 : j0 + w].rearrange("p t (c i) -> p c t i", i=WEAVE),
                ALU.subtract,
            )
            codes = keep.tile([P, w], U32, name="codes%d" % c, align_bytes=64)
            scales = keep.tile([P, w], U8, name="scales%d" % c, align_bytes=64)
            nc.vector.quantize_mx(
                out=codes[:].bitcast(FP8X4), scales=scales[:], in_=hid[:].rearrange("p w t -> p (w t)")
            )
            acc = psum.tile([P, w], F32, name="acc%d" % c)
            for n0 in range(0, w, MAX_PASS):
                n1 = min(w, n0 + MAX_PASS)
                nc.tensor.matmul_mx(
                    out=acc[:, n0:n1],
                    lhsT=w2w[:].bitcast(FP4X4),
                    lhsT_scale=w2s[:],
                    rhs=codes[:, n0:n1].bitcast(FP8X4),
                    rhs_scale=scales[:, n0:n1],
                    start=True,
                    stop=True,
                )
            res = keep.tile([P, w], F32, name="res%d" % c)
            if c + 1 < len(CHUNKS):
                nc.scalar.copy(res[:], acc[:])
            else:
                nc.vector.tensor_copy(res[:], acc[:])
            nc.sync.dma_start(out=out[:, j0 : j0 + w], in_=res[:])

        for t in range(PACK):
            make_tables(t)
        for i in range(len(steps) + 3):
            if i < PACK:
                look_up_ra(i)
            if 0 <= i - 1 < len(steps):
                look_up_rb(*steps[i - 1])
            if 0 <= i - 2 < len(steps):
                square(*steps[i - 2])
            if i >= 3 and steps[i - 3][1] == PACK - 1:
                finish(steps[i - 3][0])
